import numpy as np
import ml_dtypes


def mxq(x, axis, fmt="e4m3"):
    dtype, down = {"e4m3": (ml_dtypes.float8_e4m3fn, 7), "e5m2": (ml_dtypes.float8_e5m2, 14)}[fmt]
    v = np.moveaxis(np.asarray(x, np.float32).astype(ml_dtypes.bfloat16).astype(np.float64), axis, -1)
    blocks = v.reshape(v.shape[:-1] + (-1, 32))
    amax = np.abs(blocks).max(-1, keepdims=True)
    byte = np.maximum(np.where(amax > 0, np.frexp(amax)[1] - 1 + 127, 0) - down, 1)
    scale = np.exp2(byte - 127.0)
    codes = (blocks / scale).astype(np.float32).astype(dtype).astype(np.float64)
    return np.moveaxis((codes * scale).reshape(v.shape), -1, axis)


WIDE = False


def mx_kscale(k):
    if not WIDE:
        return np.ones(k)
    levels = np.array([10, -10, 5, -5, 0])
    if k % 512:
        return np.exp2(np.random.permutation(np.resize(levels, k // 32))).repeat(32)
    a = np.empty((k // 512, 16))
    for p in range(k // 512):
        a[p, :8] = np.random.permutation(np.resize(levels, 8))
        for g in range(8):
            far = levels[np.abs(levels - a[p, g]) >= 10]
            a[p, g + 8] = far[np.random.randint(len(far))]
    return np.exp2(a.ravel()).repeat(32)


BF16 = ml_dtypes.bfloat16


def bf(x):
    return np.asarray(x, np.float32).astype(BF16)


def f64(x):
    return np.asarray(x).astype(np.float64)


E2M1 = np.array([0.0, 0.5, 1.0, 1.5, 2.0, 3.0, 4.0, 6.0, -0.0, -0.5, -1.0, -1.5, -2.0, -3.0, -4.0, -6.0])


def pack_weight(w, fmt):
    k, n = w.shape
    w = f64(bf(w)).reshape(k // 32, 32, n)
    amax = np.abs(w).max(1)
    if fmt == "e4m3":
        byte = np.frexp(amax)[1] - 1 + 127 - 7
    else:
        mant, ex = np.frexp(amax / 6.0)
        byte = np.where(mant > 0.5, ex, ex - 1) + 127
    byte = np.clip(np.where(amax > 0, byte, 1), 1, 254)
    scaled = (w * np.exp2(127.0 - byte)[:, None, :]).reshape(k, n).astype(np.float32)
    by_word = np.ascontiguousarray(scaled.reshape(k // 512, 128, 4, n).transpose(0, 1, 3, 2))
    if fmt == "e4m3":
        words = by_word.astype(ml_dtypes.float8_e4m3fn).view(np.uint8)
    else:
        c = by_word.astype(ml_dtypes.float4_e2m1fn).view(np.uint8) & 0xF
        words = c[..., 0::2] | (c[..., 1::2] << 4)
    return np.ascontiguousarray(words), np.ascontiguousarray(byte.astype(np.uint8).reshape(k // 512, 16, n))


def unpack_weight(words, scales, fmt):
    g, p, n, _ = words.shape
    if fmt == "e4m3":
        vals = np.ascontiguousarray(words).view(ml_dtypes.float8_e4m3fn).astype(np.float64)
    else:
        nib = np.empty((g, p, n, 4), np.uint8)
        nib[..., 0::2] = words & 0xF
        nib[..., 1::2] = words >> 4
        vals = E2M1[nib]
    vals = vals * np.repeat(np.exp2(scales.astype(np.float64) - 127.0), 8, axis=1)[..., None]
    return vals.transpose(0, 1, 3, 2).reshape(g * 512, n)
def pack4(w):
    words, scales = pack_weight(w, "e2m1")
    return words.reshape(words.shape[0], 128, -1), scales


def unpack4(words, scales):
    return unpack_weight(words.reshape(words.shape[0], 128, -1, 2), scales, "e2m1")


def planes(Y):
    n, m = Y.shape
    b = f64(bf(Y)).reshape(n // 32, 32, m)
    amax = np.abs(b).max(1)
    byte = np.clip(np.where(amax > 0, np.frexp(amax)[1] - 1 + 127 - 7, 1), 1, 254)
    codes = (b * np.exp2(127.0 - byte)[:, None, :]).reshape(n, m).astype(np.float32).astype(ml_dtypes.float8_e4m3fn).view(np.uint8)
    words = codes.reshape(n // 512, 128, 4, m).transpose(0, 1, 3, 2)
    return np.ascontiguousarray(words), np.ascontiguousarray(byte.astype(np.uint8).reshape(n // 512, 16, m))


B, N, M, D, F = 2, 512, 512, 512, 512


def erf(a):
    c = np.clip(a, -6.0, 6.0)
    c2 = 2.0 * c * c
    term = c.copy()
    total = c.copy()
    for n in range(1, 150):
        term *= c2
        term /= 2.0 * n + 1.0
        total += term
    r = 2.0 / np.sqrt(np.pi) * np.exp(-c * c) * total
    return np.where(np.abs(a) <= 6.0, r, np.sign(a))


def gelu_erf(t):
    return 0.5 * t * (1.0 + erf(t / np.sqrt(2.0)))


def setup_inputs():
    s = mx_kscale(D)
    t = mx_kscale(M)
    x = bf(np.random.standard_normal((B, N, D)) * s)
    y = bf(np.random.standard_normal((B, M, D)) * 0.8 * s)
    g = bf((1.0 + 0.1 * np.random.standard_normal(D)) / (s * s))
    gp = bf(np.random.standard_normal(M) * t)
    gv = bf((1.0 + 0.1 * np.random.standard_normal(M)) / t)
    wr_words, wr_scales = pack4(np.random.standard_normal((D, F)) / np.sqrt(D) / s[:, None])
    wm_words, wm_scales = pack4(np.random.standard_normal((D, F)) * 3.0 / np.sqrt(D) / s[:, None])
    return {
        "x": x,
        "y": y,
        "g": g,
        "gp": gp,
        "gv": gv,
        "wr_words": wr_words,
        "wr_scales": wr_scales,
        "wm_words": wm_words,
        "wm_scales": wm_scales,
    }


def core(x, y, g, gp, gv, wr_words, wr_scales, wm_words, wm_scales):
    x, y, g, gp, gv = f64(x), f64(y), f64(g), f64(gp), f64(gv)

    yg = y * g[None, None, :]

    xq = mxq(x, 2, "e4m3")
    gram = xq @ mxq(yg, 2, "e4m3").transpose(0, 2, 1)

    sq = np.sum(yg * y, axis=-1)

    logits = (2.0 * gram - sq[:, None, :]) / np.sqrt(D)
    e = np.exp(logits - logits.max(-1, keepdims=True))
    p = e / e.sum(-1, keepdims=True)

    pg = p * gp[None, None, :]

    v = (mxq(y, 2, "e4m3") @ unpack4(wm_words, wm_scales)) * gv[None, :, None]

    u = (xq @ unpack4(wr_words, wr_scales)) + (mxq(pg, 2, "e4m3") @ mxq(v, 1, "e4m3"))

    return gelu_erf(u)


def reference(x, y, g, gp, gv, wr_words, wr_scales, wm_words, wm_scales):
    R_out = core(x, y, g, gp, gv, wr_words, wr_scales, wm_words, wm_scales)
    words, scales = planes(np.moveaxis(R_out, 1, 0).reshape(512, -1))
    return R_out, words, scales

@@ -1,0 +1,358 @@
+import math
+from contextlib import ExitStack
+
+import concourse.mybir as mybir
+from concourse.masks import make_identity
+
+B, N, M, D, F = 2, 512, 512, 512, 512
+FLOPS = B * 4 * 2 * 512 * 512 * 512
+
+F32 = mybir.dt.float32
+BF16 = mybir.dt.bfloat16
+U32 = mybir.dt.uint32
+I32 = mybir.dt.int32
+U8 = mybir.dt.uint8
+FP8X4 = mybir.dt.float8_e4m3fn_x4
+FP4X4 = mybir.dt.float4_e2m1fn_x4
+ACT = mybir.ActivationFunctionType
+ALU = mybir.AluOpType
+AX = mybir.AxisListType
+
+P = 128
+T = 4
+ISQ = 1.0 / math.sqrt(D)
+ORDER = """
+tr_y00 Vcp_y00 qy00 tr_y01 cp_y01 gpm00 yg00 qy01 zsq00 yg01 qyg01 tr_x00 tr_x01 wm01 gpc00 cp_x00 qx00 cp_x01
+wm02 wm00 wm03 tr_y10 qx01 qyg00 zsq01 tr_y11 Vcp_y11 cp_y10 yg10 sqm00 sqm01 ws01 yg11 qy11 ws03 qyg10 gm01
+qy10 qyg11 ws00 ws02 zsq10 wm13 vi01 vi00 sqc00 qv01 sqc01 gm03 qv00 st01 tr_x10 gm00 zsq11 ws13 cp_x10 wm12
+gm02 st03 tr_x11 st00 sqm10 ws12 cp_x11 st02 mx03 ex03 wm10 mx01 ex01 mx02 ex02 mx00 rc03 sqm11 ex00 qx11
+sqc11 rc01 qx10 gm13 gm10 wm11 sqc10 rc02 pg01 rc00 pg02 gm11 ws10 pg00 pt00 pg03 gm12 st10 st11 cpp00 ws11
+st12 mx10 ex10 mx11 mx12 st13 pt01 qp00 um01 mx13 ex11 rc11 cpp01 vi11 qp01 ex12 pg11 ex13 rc10 rc13 rc12 um03
+pg10 um02 um00 pg13 pt10 ge01 qv11 ge03 pg12 pt11 vi10 cpp10 qp10 ge00 qv10 um10 um11 Vcpp11 qp11 ge02 ge10
+um12 ge11 ge12 ob01 qo01 ob00 qo00 so00 um13 ge13 ob11 ob10 qo11 qo10 so10
+"""
+
+
+def tile_visiongnnsoftgrapher_x2_kernel(
+    tc, x, y, g, gp, gv, wr_words, wr_scales, wm_words, wm_scales, out_0, out_1, out_2
+):
+    nc = tc.nc
+    with ExitStack() as ctx:
+        keep = ctx.enter_context(tc.tile_pool(name="keep", bufs=1))
+        per = ctx.enter_context(tc.tile_pool(name="per", bufs=2))
+        row = ctx.enter_context(tc.tile_pool(name="row", bufs=4))
+        p_tr = ctx.enter_context(tc.psum_pool(name="p_tr", bufs=2))
+        p_mm = ctx.enter_context(tc.psum_pool(name="p_mm", bufs=5))
+        p_sq = ctx.enter_context(tc.psum_pool(name="p_sq", bufs=1))
+        ctx.enter_context(tc.manual_schedule())
+
+        S = [{}, {}]
+
+        def load(b, name, src):
+            t = per.tile([P, T, 512], BF16, name=name, tag=name, align_bytes=64)
+            S[b][name] = t
+            v = src[b].rearrange("(p c) d -> p c d", c=T)
+            for h in range(2):
+                nc.sync.dma_start(out=t[:, 2 * h : 2 * h + 2, :], in_=v[:, 2 * h : 2 * h + 2, :])
+
+        gcol = keep.tile([P, T], BF16, name="gcol")
+        gpcol = keep.tile([P, T], BF16, name="gpcol")
+        gvcol = keep.tile([P, T], BF16, name="gvcol")
+        wsc = keep.tile([P, 2, 512], U8, name="wsc", align_bytes=64)
+        nc.vector.memset(wsc[:].rearrange("p i n -> p (i n)").bitcast(I32), 0)
+        ident = keep.tile([P, P], F32, name="ident")
+        make_identity(nc, ident[:])
+        wmw = keep.tile([P, 1024], U8, name="wmw", align_bytes=64)
+        wrw = keep.tile([P, 1024], U8, name="wrw", align_bytes=64)
+
+        def load_scales(i, sc):
+            for q in range(4):
+                nc.sync.dma_start(
+                    out=wsc[32 * q : 32 * q + 4, i, :].bitcast(I32),
+                    in_=sc[0, 4 * q : 4 * q + 4, :].bitcast(I32),
+                )
+
+        nc.scalar.dma_start(out=gcol[:], in_=g.rearrange("(p t) -> p t", t=T))
+        load(0, "y", y)
+        load(0, "x", x)
+        nc.scalar.dma_start(out=gpcol[:], in_=gp.rearrange("(p t) -> p t", t=T))
+        nc.scalar.dma_start(out=gvcol[:], in_=gv.rearrange("(p t) -> p t", t=T))
+        nc.sync.dma_start(out=wmw[:].bitcast(I32), in_=wm_words[0].bitcast(I32))
+        load_scales(0, wm_scales)
+        load(1, "y", y)
+        load(1, "x", x)
+        nc.sync.dma_start(out=wrw[:].bitcast(I32), in_=wr_words[0].bitcast(I32))
+        load_scales(1, wr_scales)
+
+        gf = keep.tile([P, T], F32, name="gf")
+        nc.vector.tensor_copy(out=gf[:], in_=gcol[:])
+        gvf = keep.tile([P, T], F32, name="gvf")
+        gpf = keep.tile([P, T], F32, name="gpf")
+        gpb = keep.tile([P, 2, P, 2], F32, name="gpb")
+
+        def gpm():
+            nc.vector.tensor_copy(out=gpf[:], in_=gpcol[:])
+            nc.vector.tensor_copy(out=gvf[:], in_=gvcol[:])
+            ps = p_sq.tile([P, T, P], F32, name="gp_ps", tag="sq")
+            for c in range(T):
+                nc.tensor.matmul(ps[:, c, :], lhsT=gpf[:, c : c + 1].to_broadcast([P, P]), rhs=ident[:], start=True, stop=True)
+            S[0]["gp_ps"] = ps
+
+        def gpc():
+            nc.vector.tensor_copy(out=gpb[:], in_=S[0]["gp_ps"][:].rearrange("p (u e) q -> p u q e", u=2))
+
+        def words_of(t):
+            return t[:].rearrange("p c d -> p (c d)").bitcast(F32)
+
+        def tr(b, name, h):
+            w = words_of(S[b][name])
+            bank = p_tr.tile([P, 2, 2, P], F32, name="tr", tag="tr")
+            for i in range(2):
+                c = 2 * h + i
+                for u in range(2):
+                    nc.tensor.transpose(bank[:, i, u, :], w[:, 256 * c + u : 256 * (c + 1) : 2], ident[:])
+            S[b]["tr_" + name, h] = bank
+
+        def cp(b, name, h, eng=0):
+            if name + "T" not in S[b]:
+                S[b][name + "T"] = per.tile([P, 2048], BF16, name=name + "T", tag=name + "T", align_bytes=64)
+            t = S[b][name + "T"]
+            (nc.vector.tensor_copy if eng else nc.scalar.copy)(
+                out=t[:].bitcast(F32)[:, 512 * h : 512 * h + 512].rearrange("p (c r u) -> p c r u", c=2, u=2),
+                in_=S[b]["tr_" + name, h][:].rearrange("p c u r -> p c r u"),
+            )
+
+        def quant(b, name, src, lo, hi):
+            key = name + "q"
+            if key not in S[b]:
+                S[b][key] = per.tile([P, 512], U32, name=key, tag=key, align_bytes=64)
+                S[b][name + "s"] = per.tile([P, 512], U8, name=name + "s", tag=name + "s", align_bytes=64)
+            nc.vector.quantize_mx(
+                out=S[b][key][:, lo:hi].bitcast(FP8X4),
+                scales=S[b][name + "s"][:, lo:hi],
+                in_=src[:, 4 * lo : 4 * hi],
+            )
+
+        def yg(b, h):
+            if "yg" not in S[b]:
+                S[b]["yg"] = per.tile([P, 2048], BF16, name="yg", tag="yg", align_bytes=64)
+            sl = slice(1024 * h, 1024 * h + 1024)
+            nc.vector.tensor_tensor(
+                out=S[b]["yg"][:, sl].rearrange("p (m t) -> p m t", t=T),
+                in0=S[b]["yT"][:, sl].rearrange("p (m t) -> p m t", t=T),
+                in1=gcol[:].unsqueeze(1).to_broadcast([P, 256, T]),
+                op=ALU.mult,
+            )
+
+        def zsq(b, h):
+            if "z" not in S[b]:
+                S[b]["z"] = per.tile([P, T, 512], F32, name="z", tag="z")
+            nc.scalar.activation(
+                out=S[b]["z"][:, :, 256 * h : 256 * h + 256],
+                in_=S[b]["yT"][:, 1024 * h : 1024 * h + 1024].rearrange("p (m t) -> p t m", t=T),
+                func=ACT.Square,
+            )
+
+        def sqm(b, h):
+            if ("sq_ps") not in S[b]:
+                S[b]["sq_ps"] = p_sq.tile([P, 512], F32, name="sq_ps", tag="sq")
+            for t in range(T):
+                nc.tensor.matmul(
+                    S[b]["sq_ps"][:, 256 * h : 256 * h + 256], lhsT=gf[:, t : t + 1].to_broadcast([P, P]),
+                    rhs=S[b]["z"][:, t, 256 * h : 256 * h + 256], start=(t == 0), stop=(t == T - 1),
+                )
+
+        def sqc(b, h, eng=0):
+            if "sqb" not in S[b]:
+                S[b]["sqb"] = per.tile([P, 512], F32, name="sqb", tag="sqb")
+            o, i = S[b]["sqb"][:, 256 * h : 256 * h + 256], S[b]["sq_ps"][:, 256 * h : 256 * h + 256]
+            if eng:
+                nc.vector.tensor_scalar_mul(out=o, in0=i, scalar1=ISQ)
+            else:
+                nc.scalar.activation(out=o, in_=i, func=ACT.Copy, scale=ISQ)
+
+        def gm(b, j):
+            ps = p_mm.tile([P, 512], F32, name="g_ps", tag="mm")
+            nc.tensor.matmul_mx(
+                out=ps[:],
+                lhsT=S[b]["xq"][:, P * j : P * j + P].bitcast(FP8X4), lhsT_scale=S[b]["xs"][:, P * j : P * j + P],
+                rhs=S[b]["ygq"][:].bitcast(FP8X4), rhs_scale=S[b]["ygs"][:],
+                start=True, stop=True,
+            )
+            S[b]["g", j] = ps
+
+        def st(b, j):
+            lg = row.tile([P, 512], F32, name="lg", tag="lg")
+            nc.vector.scalar_tensor_tensor(
+                out=lg[:], in0=S[b]["g", j][:], scalar=-2.0 * ISQ, in1=S[b]["sqb"][:], op0=ALU.mult, op1=ALU.add
+            )
+            S[b]["lg", j] = lg
+
+        def wm(b, c):
+            ps = p_mm.tile([P, 512], F32, name="w_ps", tag="mm")
+            nc.tensor.matmul_mx(
+                out=ps[:],
+                lhsT=S[b]["yq"][:, P * c : P * c + P].bitcast(FP8X4), lhsT_scale=S[b]["ys"][:, P * c : P * c + P],
+                rhs=wmw[:].bitcast(FP4X4), rhs_scale=wsc[:, 0, :],
+                start=True, stop=True,
+            )
+            S[b]["w", c] = ps
+
+        def ws(b, c):
+            if "v4" not in S[b]:
+                S[b]["v4"] = per.tile([P, T, 512], F32, name="v4", tag="v4")
+            nc.scalar.activation(out=S[b]["v4"][:, c, :], in_=S[b]["w", c][:], func=ACT.Copy, scale=gvf[:, c : c + 1])
+
+        def vi(b, h):
+            if "vb" not in S[b]:
+                S[b]["vb"] = per.tile([P, 2048], BF16, name="vb", tag="vb", align_bytes=64)
+            nc.vector.tensor_copy(
+                out=S[b]["vb"][:, 1024 * h : 1024 * h + 1024].rearrange("p (f t) -> p f t", t=T),
+                in_=S[b]["v4"][:, :, 256 * h : 256 * h + 256].rearrange("p t f -> p f t"),
+            )
+
+        def vm(b, k):
+            ps = p_mm.tile([P, T, P], F32, name="v_ps", tag="mm")
+            for c in range(T):
+                nc.tensor.matmul_mx(
+                    out=ps[:, c, :],
+                    lhsT=S[b]["yq"][:, P * c : P * c + P].bitcast(FP8X4), lhsT_scale=S[b]["ys"][:, P * c : P * c + P],
+                    rhs=wmw[:, 256 * k : 256 * k + 256].bitcast(FP4X4), rhs_scale=wsc[:, 0, P * k : P * k + P],
+                    start=True, stop=True,
+                )
+            S[b]["v", k] = ps
+
+        def vc(b, k):
+            if "vb" not in S[b]:
+                S[b]["vb"] = per.tile([P, 2048], BF16, name="vb", tag="vb", align_bytes=64)
+            nc.vector.tensor_tensor(
+                out=S[b]["vb"][:, 512 * k : 512 * k + 512].rearrange("p (f t) -> p f t", t=T),
+                in0=S[b]["v", k][:].rearrange("p t f -> p f t"),
+                in1=gvcol[:].unsqueeze(1).to_broadcast([P, P, T]),
+                op=ALU.mult,
+            )
+
+        def mx(b, j):
+            if "mn" not in S[b]:
+                S[b]["mn"] = per.tile([P, T], F32, name="mn", tag="mn")
+                S[b]["sm"] = per.tile([P, T], F32, name="sm", tag="sm")
+                S[b]["ri"] = per.tile([P, T], F32, name="ri", tag="ri")
+            nc.vector.tensor_reduce(
+                out=S[b]["mn"][:, j : j + 1], in_=S[b]["lg", j][:], axis=AX.X, op=ALU.min
+            )
+
+        def ex(b, j):
+            e = row.tile([P, 2, P, 2], F32, name="e", tag="e")
+            nc.scalar.activation(
+                out=e[:], in_=S[b]["lg", j][:].rearrange("p (u e q) -> p u q e", u=2, e=2), func=ACT.Exp,
+                scale=-1.0, bias=S[b]["mn"][:, j : j + 1], accum_out=S[b]["sm"][:, j : j + 1],
+            )
+            S[b]["e", j] = e
+
+        def rc(b, j):
+            nc.vector.reciprocal(out=S[b]["ri"][:, j : j + 1], in_=S[b]["sm"][:, j : j + 1])
+
+        def pg(b, j):
+            t = row.tile([P, 512], BF16, name="pg", tag="pg")
+            nc.vector.scalar_tensor_tensor(
+                out=t[:], in0=S[b]["e", j][:].rearrange("p u q e -> p (u q e)"), scalar=S[b]["ri"][:, j : j + 1],
+                in1=gpb[:].rearrange("p u q e -> p (u q e)"), op0=ALU.mult, op1=ALU.mult,
+            )
+            S[b]["pg", j] = t
+
+        def pt(b, h):
+            bank = p_tr.tile([P, 2, 2, P], F32, name="tr", tag="tr")
+            for i in range(2):
+                w = S[b]["pg", 2 * h + i][:].bitcast(F32)
+                for u in range(2):
+                    nc.tensor.transpose(bank[:, i, u, :], w[:, P * u : P * u + P], ident[:])
+            S[b]["tr_p", h] = bank
+
+        def um(b, j):
+            ps = p_mm.tile([P, 512], F32, name="u_ps", tag="mm")
+            nc.tensor.matmul_mx(
+                out=ps[:],
+                lhsT=S[b]["xq"][:, P * j : P * j + P].bitcast(FP8X4), lhsT_scale=S[b]["xs"][:, P * j : P * j + P],
+                rhs=wrw[:].bitcast(FP4X4), rhs_scale=wsc[:, 1, :],
+                start=True, stop=False,
+            )
+            nc.tensor.matmul_mx(
+                out=ps[:],
+                lhsT=S[b]["pq"][:, P * j : P * j + P].bitcast(FP8X4), lhsT_scale=S[b]["ps"][:, P * j : P * j + P],
+                rhs=S[b]["vq"][:].bitcast(FP8X4), rhs_scale=S[b]["vs"][:],
+                start=False, stop=True,
+            )
+            S[b]["u", j] = ps
+
+        def ge(b, j):
+            if "o" not in S[b]:
+                S[b]["o"] = per.tile([P, T, 512], F32, name="o", tag="o")
+            nc.scalar.activation(out=S[b]["o"][:, j, :], in_=S[b]["u", j][:], func=ACT.Gelu)
+            nc.sync.dma_start(
+                out=out_0[b].rearrange("(p t) f -> p t f", t=T)[:, j, :], in_=S[b]["o"][:, j, :]
+            )
+
+        def ob(b, h):
+            if "ob" not in S[b]:
+                S[b]["ob"] = per.tile([P, 2048], BF16, name="ob", tag="ob", align_bytes=64)
+            nc.vector.tensor_copy(
+                out=S[b]["ob"][:, 1024 * h : 1024 * h + 1024].rearrange("p (f t) -> p f t", t=T),
+                in_=S[b]["o"][:, :, 256 * h : 256 * h + 256].rearrange("p t f -> p f t"),
+            )
+
+        def qo(b, h):
+            quant(b, "o", S[b]["ob"], 256 * h, 256 * h + 256)
+            c0 = b * 2048 + 1024 * h
+            nc.sync.dma_start(
+                out=out_1[0].rearrange("p m t -> p (m t)")[:, c0 : c0 + 1024].bitcast(I32),
+                in_=S[b]["oq"][:, 256 * h : 256 * h + 256].bitcast(I32),
+            )
+
+        def so(b):
+            for q in range(4):
+                nc.sync.dma_start(
+                    out=out_2[0, 4 * q : 4 * q + 4, 512 * b : 512 * b + 512].bitcast(I32),
+                    in_=S[b]["os"][32 * q : 32 * q + 4, :].bitcast(I32),
+                )
+
+        steps = {
+            "tr_y": lambda b, i: tr(b, "y", i),
+            "tr_x": lambda b, i: tr(b, "x", i),
+            "cp_y": lambda b, i: cp(b, "y", i),
+            "cp_x": lambda b, i: cp(b, "x", i),
+            "Vcp_y": lambda b, i: cp(b, "y", i, 1),
+            "Vcp_x": lambda b, i: cp(b, "x", i, 1),
+            "yg": yg,
+            "zsq": zsq,
+            "qyg": lambda b, i: quant(b, "yg", S[b]["yg"], 256 * i, 256 * i + 256),
+            "qx": lambda b, i: quant(b, "x", S[b]["xT"], 256 * i, 256 * i + 256),
+            "qy": lambda b, i: quant(b, "y", S[b]["yT"], 256 * i, 256 * i + 256),
+            "sqm": sqm,
+            "sqc": sqc,
+            "Vsqc": lambda b, i: sqc(b, i, 1),
+            "st": st,
+            "wm": wm,
+            "ws": ws,
+            "vi": vi,
+            "gm": gm,
+            "vm": vm,
+            "vc": vc,
+            "qv": lambda b, i: quant(b, "v", S[b]["vb"], 256 * i, 256 * i + 256),
+            "mx": mx,
+            "ex": ex,
+            "rc": rc,
+            "pg": pg,
+            "pt": pt,
+            "cpp": lambda b, i: cp(b, "p", i),
+            "Vcpp": lambda b, i: cp(b, "p", i, 1),
+            "qp": lambda b, i: quant(b, "p", S[b]["pT"], 256 * i, 256 * i + 256),
+            "um": um,
+            "ge": ge,
+            "ob": ob,
+            "qo": qo,
+            "so": lambda b, i: so(b),
+            "gpm": lambda b, i: gpm(),
+            "gpc": lambda b, i: gpc(),
+        }
+        for step in ORDER.split():
+            steps[step[:-2]](int(step[-2]), int(step[-1]))

@@ -19,17 +19,18 @@ ALU = mybir.AluOpType
 AX = mybir.AxisListType
 
 P = 128
+WARM = 3
 T = 4
 ISQ = 1.0 / math.sqrt(D)
 ORDER = """
-tr_y00 Vcp_y00 qy00 tr_y01 cp_y01 gpm00 yg00 qy01 zsq00 yg01 qyg01 tr_x00 tr_x01 wm01 gpc00 cp_x00 qx00 cp_x01
-wm02 wm00 wm03 tr_y10 qx01 qyg00 zsq01 tr_y11 Vcp_y11 cp_y10 yg10 sqm00 sqm01 ws01 yg11 qy11 ws03 qyg10 gm01
-qy10 qyg11 ws00 ws02 zsq10 wm13 vi01 vi00 sqc00 qv01 sqc01 gm03 qv00 st01 tr_x10 gm00 zsq11 ws13 cp_x10 wm12
-gm02 st03 tr_x11 st00 sqm10 ws12 cp_x11 st02 mx03 ex03 wm10 mx01 ex01 mx02 ex02 mx00 rc03 sqm11 ex00 qx11
-sqc11 rc01 qx10 gm13 gm10 wm11 sqc10 rc02 pg01 rc00 pg02 gm11 ws10 pg00 pt00 pg03 gm12 st10 st11 cpp00 ws11
-st12 mx10 ex10 mx11 mx12 st13 pt01 qp00 um01 mx13 ex11 rc11 cpp01 vi11 qp01 ex12 pg11 ex13 rc10 rc13 rc12 um03
-pg10 um02 um00 pg13 pt10 ge01 qv11 ge03 pg12 pt11 vi10 cpp10 qp10 ge00 qv10 um10 um11 Vcpp11 qp11 ge02 ge10
-um12 ge11 ge12 ob01 qo01 ob00 qo00 so00 um13 ge13 ob11 ob10 qo11 qo10 so10
+tr_y00 Vcp_y00 tr_y01 gpm00 tr_x00 tr_x01 cp_y01 Vzsq00 qy00 cp_x00 cp_x01 yg00 yg01 tr_y10 zsq01 tr_y11
+cp_y10 cp_y11 zsq10 Wqx00 sqm00 sqm01 qyg00 qy01 qyg01 yg10 gpm01 zsq11 yg11 gm00 qy10 gpc00 wm00 qyg10 qyg11
+ws00 qy11 Vsqc00 st00 gm01 st01 wm01 ws01 wm02 gm02 gm03 mx00 ws02 wm03 tr_x10 tr_x11 ex00 mx01 st02 ws03 st03
+mx02 ex01 sqm10 sqm11 cp_x10 mx03 wm10 rc00 Vvi00 pg00 ex02 qv00 pg01 ex03 rc01 cp_x11 Wqx10 vi01 sqc10 gm10
+ws10 wm11 pg02 pg03 gm11 qv01 ws11 pt00 cpp00 st10 st11 wm12 gm12 mx10 wm13 mx11 gm13 pt01 st12 ws12 ua00 ua01
+st13 mx12 ex10 ex11 ws13 qp00 mx13 ua02 cpp01 ua03 rc10 Vvi10 ex12 pg10 um00 ex13 ge00 pg11 rc11 pt10 cpp10
+qp01 pg12 pg13 um01 ge01 qv10 um02 ge02 um03 pt11 Vvi11 ge03 ua10 ua11 qp10 qv11 um10 ge04 Vcpp11 ge10 qp11
+um11 ua12 ob00 um12 ob01 ua13 ge11 qo00 qo01 so00 um13 ge12 ge13 ge14 ob10 ob11 qo10 qo11 so10
 """
 
 
@@ -40,9 +41,9 @@ def tile_visiongnnsoftgrapher_x2_kernel(
     with ExitStack() as ctx:
         keep = ctx.enter_context(tc.tile_pool(name="keep", bufs=1))
         per = ctx.enter_context(tc.tile_pool(name="per", bufs=2))
-        row = ctx.enter_context(tc.tile_pool(name="row", bufs=4))
-        p_tr = ctx.enter_context(tc.psum_pool(name="p_tr", bufs=2))
-        p_mm = ctx.enter_context(tc.psum_pool(name="p_mm", bufs=5))
+        row = ctx.enter_context(tc.tile_pool(name="row", bufs=8))
+        p_tr = ctx.enter_context(tc.psum_pool(name="p_tr", bufs=3))
+        p_mm = ctx.enter_context(tc.psum_pool(name="p_mm", bufs=4))
         p_sq = ctx.enter_context(tc.psum_pool(name="p_sq", bufs=1))
         ctx.enter_context(tc.manual_schedule())
 
@@ -72,34 +73,44 @@ def tile_visiongnnsoftgrapher_x2_kernel(
                     in_=sc[0, 4 * q : 4 * q + 4, :].bitcast(I32),
                 )
 
+        nc.scalar.dma_start(out=gpcol[:], in_=gp.rearrange("(p t) -> p t", t=T))
         nc.scalar.dma_start(out=gcol[:], in_=g.rearrange("(p t) -> p t", t=T))
+        nc.scalar.dma_start(out=gvcol[:], in_=gv.rearrange("(p t) -> p t", t=T))
         load(0, "y", y)
         load(0, "x", x)
-        nc.scalar.dma_start(out=gpcol[:], in_=gp.rearrange("(p t) -> p t", t=T))
-        nc.scalar.dma_start(out=gvcol[:], in_=gv.rearrange("(p t) -> p t", t=T))
-        nc.sync.dma_start(out=wmw[:].bitcast(I32), in_=wm_words[0].bitcast(I32))
-        load_scales(0, wm_scales)
         load(1, "y", y)
         load(1, "x", x)
+        nc.sync.dma_start(out=wmw[:].bitcast(I32), in_=wm_words[0].bitcast(I32))
         nc.sync.dma_start(out=wrw[:].bitcast(I32), in_=wr_words[0].bitcast(I32))
+        load_scales(0, wm_scales)
         load_scales(1, wr_scales)
 
+        for w in range(WARM):
+            warm = p_tr.tile([P, P], F32, name="warm", tag="tr")
+            nc.tensor.matmul(warm[:], lhsT=ident[:], rhs=ident[:], start=True, stop=True)
+
+        gpf = keep.tile([P, T], F32, name="gpf")
+        nc.vector.tensor_copy(out=gpf[:], in_=gpcol[:])
         gf = keep.tile([P, T], F32, name="gf")
         nc.vector.tensor_copy(out=gf[:], in_=gcol[:])
         gvf = keep.tile([P, T], F32, name="gvf")
-        gpf = keep.tile([P, T], F32, name="gpf")
+        nc.vector.tensor_copy(out=gvf[:], in_=gvcol[:])
         gpb = keep.tile([P, 2, P, 2], F32, name="gpb")
 
-        def gpm():
-            nc.vector.tensor_copy(out=gpf[:], in_=gpcol[:])
-            nc.vector.tensor_copy(out=gvf[:], in_=gvcol[:])
-            ps = p_sq.tile([P, T, P], F32, name="gp_ps", tag="sq")
-            for c in range(T):
-                nc.tensor.matmul(ps[:, c, :], lhsT=gpf[:, c : c + 1].to_broadcast([P, P]), rhs=ident[:], start=True, stop=True)
-            S[0]["gp_ps"] = ps
+        def gpm(h):
+            if h == 0:
+                S[0]["gp_ps"] = p_mm.tile([P, T, P], F32, name="gp_ps", tag="mm")
+            for c in (2 * h, 2 * h + 1):
+                nc.tensor.matmul(
+                    S[0]["gp_ps"][:, c, :], lhsT=gpf[:, c : c + 1].to_broadcast([P, P]), rhs=ident[:], start=True, stop=True
+                )
 
-        def gpc():
-            nc.vector.tensor_copy(out=gpb[:], in_=S[0]["gp_ps"][:].rearrange("p (u e) q -> p u q e", u=2))
+        def gpc(eng):
+            o, i = gpb[:], S[0]["gp_ps"][:].rearrange("p (u e) q -> p u q e", u=2)
+            if eng:
+                nc.vector.tensor_copy(out=o, in_=i)
+            else:
+                nc.scalar.copy(out=o, in_=i)
 
         def words_of(t):
             return t[:].rearrange("p c d -> p (c d)").bitcast(F32)
@@ -144,14 +155,17 @@ def tile_visiongnnsoftgrapher_x2_kernel(
                 op=ALU.mult,
             )
 
-        def zsq(b, h):
+        def zsq(b, h, eng=0):
             if "z" not in S[b]:
                 S[b]["z"] = per.tile([P, T, 512], F32, name="z", tag="z")
-            nc.scalar.activation(
-                out=S[b]["z"][:, :, 256 * h : 256 * h + 256],
-                in_=S[b]["yT"][:, 1024 * h : 1024 * h + 1024].rearrange("p (m t) -> p t m", t=T),
-                func=ACT.Square,
-            )
+            o = S[b]["z"][:, :, 256 * h : 256 * h + 256]
+            i = S[b]["yT"][:, 1024 * h : 1024 * h + 1024].rearrange("p (m t) -> p t m", t=T)
+            if eng == 0:
+                nc.scalar.activation(out=o, in_=i, func=ACT.Square)
+            elif eng == 1:
+                nc.vector.tensor_tensor(out=o, in0=i, in1=i, op=ALU.mult)
+            else:
+                nc.gpsimd.tensor_tensor(out=o, in0=i, in1=i, op=ALU.mult)
 
         def sqm(b, h):
             if ("sq_ps") not in S[b]:
@@ -165,7 +179,7 @@ def tile_visiongnnsoftgrapher_x2_kernel(
         def sqc(b, h, eng=0):
             if "sqb" not in S[b]:
                 S[b]["sqb"] = per.tile([P, 512], F32, name="sqb", tag="sqb")
-            o, i = S[b]["sqb"][:, 256 * h : 256 * h + 256], S[b]["sq_ps"][:, 256 * h : 256 * h + 256]
+            o, i = S[b]["sqb"][:], S[b]["sq_ps"][:]
             if eng:
                 nc.vector.tensor_scalar_mul(out=o, in0=i, scalar1=ISQ)
             else:
@@ -203,13 +217,16 @@ def tile_visiongnnsoftgrapher_x2_kernel(
                 S[b]["v4"] = per.tile([P, T, 512], F32, name="v4", tag="v4")
             nc.scalar.activation(out=S[b]["v4"][:, c, :], in_=S[b]["w", c][:], func=ACT.Copy, scale=gvf[:, c : c + 1])
 
-        def vi(b, h):
+        def vi(b, i, parts, eng):
             if "vb" not in S[b]:
                 S[b]["vb"] = per.tile([P, 2048], BF16, name="vb", tag="vb", align_bytes=64)
-            nc.vector.tensor_copy(
-                out=S[b]["vb"][:, 1024 * h : 1024 * h + 1024].rearrange("p (f t) -> p f t", t=T),
-                in_=S[b]["v4"][:, :, 256 * h : 256 * h + 256].rearrange("p t f -> p f t"),
-            )
+            w = 512 // parts
+            o = S[b]["vb"][:, T * w * i : T * w * (i + 1)].rearrange("p (f t) -> p f t", t=T)
+            s = S[b]["v4"][:, :, w * i : w * (i + 1)].rearrange("p t f -> p f t")
+            if eng:
+                nc.vector.tensor_copy(out=o, in_=s)
+            else:
+                nc.scalar.copy(out=o, in_=s)
 
         def vm(b, k):
             ps = p_mm.tile([P, T, P], F32, name="v_ps", tag="mm")
@@ -249,8 +266,9 @@ def tile_visiongnnsoftgrapher_x2_kernel(
             )
             S[b]["e", j] = e
 
-        def rc(b, j):
-            nc.vector.reciprocal(out=S[b]["ri"][:, j : j + 1], in_=S[b]["sm"][:, j : j + 1])
+        def rc(b, h):
+            sl = slice(2 * h, 2 * h + 2)
+            nc.vector.reciprocal(out=S[b]["ri"][:, sl], in_=S[b]["sm"][:, sl])
 
         def pg(b, j):
             t = row.tile([P, 512], BF16, name="pg", tag="pg")
@@ -268,7 +286,7 @@ def tile_visiongnnsoftgrapher_x2_kernel(
                     nc.tensor.transpose(bank[:, i, u, :], w[:, P * u : P * u + P], ident[:])
             S[b]["tr_p", h] = bank
 
-        def um(b, j):
+        def ua(b, j):
             ps = p_mm.tile([P, 512], F32, name="u_ps", tag="mm")
             nc.tensor.matmul_mx(
                 out=ps[:],
@@ -276,20 +294,26 @@ def tile_visiongnnsoftgrapher_x2_kernel(
                 rhs=wrw[:].bitcast(FP4X4), rhs_scale=wsc[:, 1, :],
                 start=True, stop=False,
             )
+            S[b]["u", j] = ps
+
+        def um(b, j):
             nc.tensor.matmul_mx(
-                out=ps[:],
+                out=S[b]["u", j][:],
                 lhsT=S[b]["pq"][:, P * j : P * j + P].bitcast(FP8X4), lhsT_scale=S[b]["ps"][:, P * j : P * j + P],
                 rhs=S[b]["vq"][:].bitcast(FP8X4), rhs_scale=S[b]["vs"][:],
                 start=False, stop=True,
             )
-            S[b]["u", j] = ps
 
-        def ge(b, j):
+        def ge(b, i):
             if "o" not in S[b]:
                 S[b]["o"] = per.tile([P, T, 512], F32, name="o", tag="o")
-            nc.scalar.activation(out=S[b]["o"][:, j, :], in_=S[b]["u", j][:], func=ACT.Gelu)
+            if i < 3:
+                j, sl = i, slice(0, 512)
+            else:
+                j, sl = 3, slice(256 * (i - 3), 256 * (i - 3) + 256)
+            nc.scalar.activation(out=S[b]["o"][:, j, sl], in_=S[b]["u", j][:, sl], func=ACT.Gelu)
             nc.sync.dma_start(
-                out=out_0[b].rearrange("(p t) f -> p t f", t=T)[:, j, :], in_=S[b]["o"][:, j, :]
+                out=out_0[b].rearrange("(p t) f -> p t f", t=T)[:, j, sl], in_=S[b]["o"][:, j, sl]
             )
 
         def ob(b, h):
@@ -324,7 +348,11 @@ def tile_visiongnnsoftgrapher_x2_kernel(
             "Vcp_x": lambda b, i: cp(b, "x", i, 1),
             "yg": yg,
             "zsq": zsq,
+            "Vzsq": lambda b, i: zsq(b, i, 1),
+            "Gzsq": lambda b, i: zsq(b, i, 2),
             "qyg": lambda b, i: quant(b, "yg", S[b]["yg"], 256 * i, 256 * i + 256),
+            "Wqx": lambda b, i: quant(b, "x", S[b]["xT"], 0, 512),
+            "Wqy": lambda b, i: quant(b, "y", S[b]["yT"], 0, 512),
             "qx": lambda b, i: quant(b, "x", S[b]["xT"], 256 * i, 256 * i + 256),
             "qy": lambda b, i: quant(b, "y", S[b]["yT"], 256 * i, 256 * i + 256),
             "sqm": sqm,
@@ -333,7 +361,8 @@ def tile_visiongnnsoftgrapher_x2_kernel(
             "st": st,
             "wm": wm,
             "ws": ws,
-            "vi": vi,
+            "vi": lambda b, i: vi(b, i, 2, 0),
+            "Vvi": lambda b, i: vi(b, i, 2, 1),
             "gm": gm,
             "vm": vm,
             "vc": vc,
@@ -346,13 +375,15 @@ def tile_visiongnnsoftgrapher_x2_kernel(
             "cpp": lambda b, i: cp(b, "p", i),
             "Vcpp": lambda b, i: cp(b, "p", i, 1),
             "qp": lambda b, i: quant(b, "p", S[b]["pT"], 256 * i, 256 * i + 256),
+            "ua": ua,
             "um": um,
             "ge": ge,
             "ob": ob,
             "qo": qo,
             "so": lambda b, i: so(b),
-            "gpm": lambda b, i: gpm(),
-            "gpc": lambda b, i: gpc(),
+            "gpm": lambda b, i: gpm(i),
+            "gpc": lambda b, i: gpc(0),
+            "Vgpc": lambda b, i: gpc(1),
         }
         for step in ORDER.split():
             steps[step[:-2]](int(step[-2]), int(step[-1]))

import math
from contextlib import ExitStack

import concourse.mybir as mybir
from concourse.masks import make_identity

B, N, M, D, F = 2, 512, 512, 512, 512
FLOPS = B * 4 * 2 * 512 * 512 * 512

F32 = mybir.dt.float32
BF16 = mybir.dt.bfloat16
U32 = mybir.dt.uint32
I32 = mybir.dt.int32
U8 = mybir.dt.uint8
FP8X4 = mybir.dt.float8_e4m3fn_x4
FP4X4 = mybir.dt.float4_e2m1fn_x4
ACT = mybir.ActivationFunctionType
ALU = mybir.AluOpType
AX = mybir.AxisListType

P = 128
WARM = 3
T = 4
ISQ = 1.0 / math.sqrt(D)
ORDER = """
tr_y00 Vcp_y00 tr_y01 gpm00 tr_x00 tr_x01 cp_y01 Vzsq00 qy00 cp_x00 cp_x01 yg00 yg01 tr_y10 zsq01 tr_y11
cp_y10 cp_y11 zsq10 Wqx00 sqm00 sqm01 qyg00 qy01 qyg01 yg10 gpm01 zsq11 yg11 gm00 qy10 gpc00 wm00 qyg10 qyg11
ws00 qy11 Vsqc00 st00 gm01 st01 wm01 ws01 wm02 gm02 gm03 mx00 ws02 wm03 tr_x10 tr_x11 ex00 mx01 st02 ws03 st03
mx02 ex01 sqm10 sqm11 cp_x10 mx03 wm10 rc00 Vvi00 pg00 ex02 qv00 pg01 ex03 rc01 cp_x11 Wqx10 vi01 sqc10 gm10
ws10 wm11 pg02 pg03 gm11 qv01 ws11 pt00 cpp00 st10 st11 wm12 gm12 mx10 wm13 mx11 gm13 pt01 st12 ws12 ua00 ua01
st13 mx12 ex10 ex11 ws13 qp00 mx13 ua02 cpp01 ua03 rc10 Vvi10 ex12 pg10 um00 ex13 ge00 pg11 rc11 pt10 cpp10
qp01 pg12 pg13 um01 ge01 qv10 um02 ge02 um03 pt11 Vvi11 ge03 ua10 ua11 qp10 qv11 um10 ge04 Vcpp11 ge10 qp11
um11 ua12 ob00 um12 ob01 ua13 ge11 qo00 qo01 so00 um13 ge12 ge13 ge14 ob10 ob11 qo10 qo11 so10
"""


def tile_visiongnnsoftgrapher_x2_kernel(
    tc, x, y, g, gp, gv, wr_words, wr_scales, wm_words, wm_scales, out_0, out_1, out_2
):
    nc = tc.nc
    with ExitStack() as ctx:
        keep = ctx.enter_context(tc.tile_pool(name="keep", bufs=1))
        per = ctx.enter_context(tc.tile_pool(name="per", bufs=2))
        row = ctx.enter_context(tc.tile_pool(name="row", bufs=8))
        p_tr = ctx.enter_context(tc.psum_pool(name="p_tr", bufs=3))
        p_mm = ctx.enter_context(tc.psum_pool(name="p_mm", bufs=4))
        p_sq = ctx.enter_context(tc.psum_pool(name="p_sq", bufs=1))
        ctx.enter_context(tc.manual_schedule())

        S = [{}, {}]

        def load(b, name, src):
            t = per.tile([P, T, 512], BF16, name=name, tag=name, align_bytes=64)
            S[b][name] = t
            v = src[b].rearrange("(p c) d -> p c d", c=T)
            for h in range(2):
                nc.sync.dma_start(out=t[:, 2 * h : 2 * h + 2, :], in_=v[:, 2 * h : 2 * h + 2, :])

        gcol = keep.tile([P, T], BF16, name="gcol")
        gpcol = keep.tile([P, T], BF16, name="gpcol")
        gvcol = keep.tile([P, T], BF16, name="gvcol")
        wsc = keep.tile([P, 2, 512], U8, name="wsc", align_bytes=64)
        nc.vector.memset(wsc[:].rearrange("p i n -> p (i n)").bitcast(I32), 0)
        ident = keep.tile([P, P], F32, name="ident")
        make_identity(nc, ident[:])
        wmw = keep.tile([P, 1024], U8, name="wmw", align_bytes=64)
        wrw = keep.tile([P, 1024], U8, name="wrw", align_bytes=64)

        def load_scales(i, sc):
            for q in range(4):
                nc.sync.dma_start(
                    out=wsc[32 * q : 32 * q + 4, i, :].bitcast(I32),
                    in_=sc[0, 4 * q : 4 * q + 4, :].bitcast(I32),
                )

        nc.scalar.dma_start(out=gpcol[:], in_=gp.rearrange("(p t) -> p t", t=T))
        nc.scalar.dma_start(out=gcol[:], in_=g.rearrange("(p t) -> p t", t=T))
        nc.scalar.dma_start(out=gvcol[:], in_=gv.rearrange("(p t) -> p t", t=T))
        load(0, "y", y)
        load(0, "x", x)
        load(1, "y", y)
        load(1, "x", x)
        nc.sync.dma_start(out=wmw[:].bitcast(I32), in_=wm_words[0].bitcast(I32))
        nc.sync.dma_start(out=wrw[:].bitcast(I32), in_=wr_words[0].bitcast(I32))
        load_scales(0, wm_scales)
        load_scales(1, wr_scales)

        for w in range(WARM):
            warm = p_tr.tile([P, P], F32, name="warm", tag="tr")
            nc.tensor.matmul(warm[:], lhsT=ident[:], rhs=ident[:], start=True, stop=True)

        gpf = keep.tile([P, T], F32, name="gpf")
        nc.vector.tensor_copy(out=gpf[:], in_=gpcol[:])
        gf = keep.tile([P, T], F32, name="gf")
        nc.vector.tensor_copy(out=gf[:], in_=gcol[:])
        gvf = keep.tile([P, T], F32, name="gvf")
        nc.vector.tensor_copy(out=gvf[:], in_=gvcol[:])
        gpb = keep.tile([P, 2, P, 2], F32, name="gpb")

        def gpm(h):
            if h == 0:
                S[0]["gp_ps"] = p_mm.tile([P, T, P], F32, name="gp_ps", tag="mm")
            for c in (2 * h, 2 * h + 1):
                nc.tensor.matmul(
                    S[0]["gp_ps"][:, c, :], lhsT=gpf[:, c : c + 1].to_broadcast([P, P]), rhs=ident[:], start=True, stop=True
                )

        def gpc(eng):
            o, i = gpb[:], S[0]["gp_ps"][:].rearrange("p (u e) q -> p u q e", u=2)
            if eng:
                nc.vector.tensor_copy(out=o, in_=i)
            else:
                nc.scalar.copy(out=o, in_=i)

        def words_of(t):
            return t[:].rearrange("p c d -> p (c d)").bitcast(F32)

        def tr(b, name, h):
            w = words_of(S[b][name])
            bank = p_tr.tile([P, 2, 2, P], F32, name="tr", tag="tr")
            for i in range(2):
                c = 2 * h + i
                for u in range(2):
                    nc.tensor.transpose(bank[:, i, u, :], w[:, 256 * c + u : 256 * (c + 1) : 2], ident[:])
            S[b]["tr_" + name, h] = bank

        def cp(b, name, h, eng=0):
            if name + "T" not in S[b]:
                S[b][name + "T"] = per.tile([P, 2048], BF16, name=name + "T", tag=name + "T", align_bytes=64)
            t = S[b][name + "T"]
            (nc.vector.tensor_copy if eng else nc.scalar.copy)(
                out=t[:].bitcast(F32)[:, 512 * h : 512 * h + 512].rearrange("p (c r u) -> p c r u", c=2, u=2),
                in_=S[b]["tr_" + name, h][:].rearrange("p c u r -> p c r u"),
            )

        def quant(b, name, src, lo, hi):
            key = name + "q"
            if key not in S[b]:
                S[b][key] = per.tile([P, 512], U32, name=key, tag=key, align_bytes=64)
                S[b][name + "s"] = per.tile([P, 512], U8, name=name + "s", tag=name + "s", align_bytes=64)
            nc.vector.quantize_mx(
                out=S[b][key][:, lo:hi].bitcast(FP8X4),
                scales=S[b][name + "s"][:, lo:hi],
                in_=src[:, 4 * lo : 4 * hi],
            )

        def yg(b, h):
            if "yg" not in S[b]:
                S[b]["yg"] = per.tile([P, 2048], BF16, name="yg", tag="yg", align_bytes=64)
            sl = slice(1024 * h, 1024 * h + 1024)
            nc.vector.tensor_tensor(
                out=S[b]["yg"][:, sl].rearrange("p (m t) -> p m t", t=T),
                in0=S[b]["yT"][:, sl].rearrange("p (m t) -> p m t", t=T),
                in1=gcol[:].unsqueeze(1).to_broadcast([P, 256, T]),
                op=ALU.mult,
            )

        def zsq(b, h, eng=0):
            if "z" not in S[b]:
                S[b]["z"] = per.tile([P, T, 512], F32, name="z", tag="z")
            o = S[b]["z"][:, :, 256 * h : 256 * h + 256]
            i = S[b]["yT"][:, 1024 * h : 1024 * h + 1024].rearrange("p (m t) -> p t m", t=T)
            if eng == 0:
                nc.scalar.activation(out=o, in_=i, func=ACT.Square)
            elif eng == 1:
                nc.vector.tensor_tensor(out=o, in0=i, in1=i, op=ALU.mult)
            else:
                nc.gpsimd.tensor_tensor(out=o, in0=i, in1=i, op=ALU.mult)

        def sqm(b, h):
            if ("sq_ps") not in S[b]:
                S[b]["sq_ps"] = p_sq.tile([P, 512], F32, name="sq_ps", tag="sq")
            for t in range(T):
                nc.tensor.matmul(
                    S[b]["sq_ps"][:, 256 * h : 256 * h + 256], lhsT=gf[:, t : t + 1].to_broadcast([P, P]),
                    rhs=S[b]["z"][:, t, 256 * h : 256 * h + 256], start=(t == 0), stop=(t == T - 1),
                )

        def sqc(b, h, eng=0):
            if "sqb" not in S[b]:
                S[b]["sqb"] = per.tile([P, 512], F32, name="sqb", tag="sqb")
            o, i = S[b]["sqb"][:], S[b]["sq_ps"][:]
            if eng:
                nc.vector.tensor_scalar_mul(out=o, in0=i, scalar1=ISQ)
            else:
                nc.scalar.activation(out=o, in_=i, func=ACT.Copy, scale=ISQ)

        def gm(b, j):
            ps = p_mm.tile([P, 512], F32, name="g_ps", tag="mm")
            nc.tensor.matmul_mx(
                out=ps[:],
                lhsT=S[b]["xq"][:, P * j : P * j + P].bitcast(FP8X4), lhsT_scale=S[b]["xs"][:, P * j : P * j + P],
                rhs=S[b]["ygq"][:].bitcast(FP8X4), rhs_scale=S[b]["ygs"][:],
                start=True, stop=True,
            )
            S[b]["g", j] = ps

        def st(b, j):
            lg = row.tile([P, 512], F32, name="lg", tag="lg")
            nc.vector.scalar_tensor_tensor(
                out=lg[:], in0=S[b]["g", j][:], scalar=-2.0 * ISQ, in1=S[b]["sqb"][:], op0=ALU.mult, op1=ALU.add
            )
            S[b]["lg", j] = lg

        def wm(b, c):
            ps = p_mm.tile([P, 512], F32, name="w_ps", tag="mm")
            nc.tensor.matmul_mx(
                out=ps[:],
                lhsT=S[b]["yq"][:, P * c : P * c + P].bitcast(FP8X4), lhsT_scale=S[b]["ys"][:, P * c : P * c + P],
                rhs=wmw[:].bitcast(FP4X4), rhs_scale=wsc[:, 0, :],
                start=True, stop=True,
            )
            S[b]["w", c] = ps

        def ws(b, c):
            if "v4" not in S[b]:
                S[b]["v4"] = per.tile([P, T, 512], F32, name="v4", tag="v4")
            nc.scalar.activation(out=S[b]["v4"][:, c, :], in_=S[b]["w", c][:], func=ACT.Copy, scale=gvf[:, c : c + 1])

        def vi(b, i, parts, eng):
            if "vb" not in S[b]:
                S[b]["vb"] = per.tile([P, 2048], BF16, name="vb", tag="vb", align_bytes=64)
            w = 512 // parts
            o = S[b]["vb"][:, T * w * i : T * w * (i + 1)].rearrange("p (f t) -> p f t", t=T)
            s = S[b]["v4"][:, :, w * i : w * (i + 1)].rearrange("p t f -> p f t")
            if eng:
                nc.vector.tensor_copy(out=o, in_=s)
            else:
                nc.scalar.copy(out=o, in_=s)

        def vm(b, k):
            ps = p_mm.tile([P, T, P], F32, name="v_ps", tag="mm")
            for c in range(T):
                nc.tensor.matmul_mx(
                    out=ps[:, c, :],
                    lhsT=S[b]["yq"][:, P * c : P * c + P].bitcast(FP8X4), lhsT_scale=S[b]["ys"][:, P * c : P * c + P],
                    rhs=wmw[:, 256 * k : 256 * k + 256].bitcast(FP4X4), rhs_scale=wsc[:, 0, P * k : P * k + P],
                    start=True, stop=True,
                )
            S[b]["v", k] = ps

        def vc(b, k):
            if "vb" not in S[b]:
                S[b]["vb"] = per.tile([P, 2048], BF16, name="vb", tag="vb", align_bytes=64)
            nc.vector.tensor_tensor(
                out=S[b]["vb"][:, 512 * k : 512 * k + 512].rearrange("p (f t) -> p f t", t=T),
                in0=S[b]["v", k][:].rearrange("p t f -> p f t"),
                in1=gvcol[:].unsqueeze(1).to_broadcast([P, P, T]),
                op=ALU.mult,
            )

        def mx(b, j):
            if "mn" not in S[b]:
                S[b]["mn"] = per.tile([P, T], F32, name="mn", tag="mn")
                S[b]["sm"] = per.tile([P, T], F32, name="sm", tag="sm")
                S[b]["ri"] = per.tile([P, T], F32, name="ri", tag="ri")
            nc.vector.tensor_reduce(
                out=S[b]["mn"][:, j : j + 1], in_=S[b]["lg", j][:], axis=AX.X, op=ALU.min
            )

        def ex(b, j):
            e = row.tile([P, 2, P, 2], F32, name="e", tag="e")
            nc.scalar.activation(
                out=e[:], in_=S[b]["lg", j][:].rearrange("p (u e q) -> p u q e", u=2, e=2), func=ACT.Exp,
                scale=-1.0, bias=S[b]["mn"][:, j : j + 1], accum_out=S[b]["sm"][:, j : j + 1],
            )
            S[b]["e", j] = e

        def rc(b, h):
            sl = slice(2 * h, 2 * h + 2)
            nc.vector.reciprocal(out=S[b]["ri"][:, sl], in_=S[b]["sm"][:, sl])

        def pg(b, j):
            t = row.tile([P, 512], BF16, name="pg", tag="pg")
            nc.vector.scalar_tensor_tensor(
                out=t[:], in0=S[b]["e", j][:].rearrange("p u q e -> p (u q e)"), scalar=S[b]["ri"][:, j : j + 1],
                in1=gpb[:].rearrange("p u q e -> p (u q e)"), op0=ALU.mult, op1=ALU.mult,
            )
            S[b]["pg", j] = t

        def pt(b, h):
            bank = p_tr.tile([P, 2, 2, P], F32, name="tr", tag="tr")
            for i in range(2):
                w = S[b]["pg", 2 * h + i][:].bitcast(F32)
                for u in range(2):
                    nc.tensor.transpose(bank[:, i, u, :], w[:, P * u : P * u + P], ident[:])
            S[b]["tr_p", h] = bank

        def ua(b, j):
            ps = p_mm.tile([P, 512], F32, name="u_ps", tag="mm")
            nc.tensor.matmul_mx(
                out=ps[:],
                lhsT=S[b]["xq"][:, P * j : P * j + P].bitcast(FP8X4), lhsT_scale=S[b]["xs"][:, P * j : P * j + P],
                rhs=wrw[:].bitcast(FP4X4), rhs_scale=wsc[:, 1, :],
                start=True, stop=False,
            )
            S[b]["u", j] = ps

        def um(b, j):
            nc.tensor.matmul_mx(
                out=S[b]["u", j][:],
                lhsT=S[b]["pq"][:, P * j : P * j + P].bitcast(FP8X4), lhsT_scale=S[b]["ps"][:, P * j : P * j + P],
                rhs=S[b]["vq"][:].bitcast(FP8X4), rhs_scale=S[b]["vs"][:],
                start=False, stop=True,
            )

        def ge(b, i):
            if "o" not in S[b]:
                S[b]["o"] = per.tile([P, T, 512], F32, name="o", tag="o")
            if i < 3:
                j, sl = i, slice(0, 512)
            else:
                j, sl = 3, slice(256 * (i - 3), 256 * (i - 3) + 256)
            nc.scalar.activation(out=S[b]["o"][:, j, sl], in_=S[b]["u", j][:, sl], func=ACT.Gelu)
            nc.sync.dma_start(
                out=out_0[b].rearrange("(p t) f -> p t f", t=T)[:, j, sl], in_=S[b]["o"][:, j, sl]
            )

        def ob(b, h):
            if "ob" not in S[b]:
                S[b]["ob"] = per.tile([P, 2048], BF16, name="ob", tag="ob", align_bytes=64)
            nc.vector.tensor_copy(
                out=S[b]["ob"][:, 1024 * h : 1024 * h + 1024].rearrange("p (f t) -> p f t", t=T),
                in_=S[b]["o"][:, :, 256 * h : 256 * h + 256].rearrange("p t f -> p f t"),
            )

        def qo(b, h):
            quant(b, "o", S[b]["ob"], 256 * h, 256 * h + 256)
            c0 = b * 2048 + 1024 * h
            nc.sync.dma_start(
                out=out_1[0].rearrange("p m t -> p (m t)")[:, c0 : c0 + 1024].bitcast(I32),
                in_=S[b]["oq"][:, 256 * h : 256 * h + 256].bitcast(I32),
            )

        def so(b):
            for q in range(4):
                nc.sync.dma_start(
                    out=out_2[0, 4 * q : 4 * q + 4, 512 * b : 512 * b + 512].bitcast(I32),
                    in_=S[b]["os"][32 * q : 32 * q + 4, :].bitcast(I32),
                )

        steps = {
            "tr_y": lambda b, i: tr(b, "y", i),
            "tr_x": lambda b, i: tr(b, "x", i),
            "cp_y": lambda b, i: cp(b, "y", i),
            "cp_x": lambda b, i: cp(b, "x", i),
            "Vcp_y": lambda b, i: cp(b, "y", i, 1),
            "Vcp_x": lambda b, i: cp(b, "x", i, 1),
            "yg": yg,
            "zsq": zsq,
            "Vzsq": lambda b, i: zsq(b, i, 1),
            "Gzsq": lambda b, i: zsq(b, i, 2),
            "qyg": lambda b, i: quant(b, "yg", S[b]["yg"], 256 * i, 256 * i + 256),
            "Wqx": lambda b, i: quant(b, "x", S[b]["xT"], 0, 512),
            "Wqy": lambda b, i: quant(b, "y", S[b]["yT"], 0, 512),
            "qx": lambda b, i: quant(b, "x", S[b]["xT"], 256 * i, 256 * i + 256),
            "qy": lambda b, i: quant(b, "y", S[b]["yT"], 256 * i, 256 * i + 256),
            "sqm": sqm,
            "sqc": sqc,
            "Vsqc": lambda b, i: sqc(b, i, 1),
            "st": st,
            "wm": wm,
            "ws": ws,
            "vi": lambda b, i: vi(b, i, 2, 0),
            "Vvi": lambda b, i: vi(b, i, 2, 1),
            "gm": gm,
            "vm": vm,
            "vc": vc,
            "qv": lambda b, i: quant(b, "v", S[b]["vb"], 256 * i, 256 * i + 256),
            "mx": mx,
            "ex": ex,
            "rc": rc,
            "pg": pg,
            "pt": pt,
            "cpp": lambda b, i: cp(b, "p", i),
            "Vcpp": lambda b, i: cp(b, "p", i, 1),
            "qp": lambda b, i: quant(b, "p", S[b]["pT"], 256 * i, 256 * i + 256),
            "ua": ua,
            "um": um,
            "ge": ge,
            "ob": ob,
            "qo": qo,
            "so": lambda b, i: so(b),
            "gpm": lambda b, i: gpm(i),
            "gpc": lambda b, i: gpc(0),
            "Vgpc": lambda b, i: gpc(1),
        }
        for step in ORDER.split():
            steps[step[:-2]](int(step[-2]), int(step[-1]))
